import numpy as np, ml_dtypes
CORES = [66,74,82,90,194,202,210,218]
N = 8
import mx_ref
NC, G = 128, 4
C = np.float32(2.0 ** -4)
CNT = [[0,24,32,4,32,0,0,36],[16,0,0,8,0,72,24,8],[8,4,0,96,0,0,4,16],[28,32,0,0,8,0,44,16],[28,0,32,0,0,16,24,28],[8,0,32,0,64,0,0,24],[24,36,32,0,0,36,0,0],[16,32,0,20,24,4,32,0]]
OFF = [[sum(c[:e]) for e in range(N + 1)] for c in CNT]
BF = ml_dtypes.bfloat16
def cut(t, i, w=512):
    return t[:, w * i:w * i + w]
def tile(rs):
    return np.stack(rs, axis=2).reshape(128, -1).astype(BF)
def layer(w, X):
    out = []
    for i in range(G):
        for t in range(len(X)):
            p = mx_ref.matmul(mx_ref.quantize(cut(w, len(X) * i + t)), X[t])
            z = p if t == 0 else z + p
        out.append(z)
    return out
def gated(Z, g):
    return [(np.maximum(z, 0) * C) * g for z in Z]
def setup_inputs(rng):
    def f(*shape):
        return mx_ref.flush((rng.standard_normal(shape, dtype=np.float32) * np.exp2(rng.integers(-2, 3, shape[:-1] + (1,)))).astype(BF))
    gt = np.broadcast_to((0.125 + 0.875 * rng.random((N, 1, NC))).astype(BF), (N, 128, NC)).copy()
    return {"gt": gt, "x": f(N, 128, 4 * NC), "w1": f(N, 128, G * 512), "w2": f(N, 128, 512)}
def setup_inputs_blocks(rng):
    d = setup_inputs(rng)
    for k in ("x", "w1", "w2"): d[k] = mx_ref.spread(d[k], rng, 4)
    return d
def setup_inputs_wide(rng):
    d = setup_inputs(rng)
    for k in ("x", "w1", "w2"): d[k] = mx_ref.flush((d[k].astype(np.float32) * np.exp2(rng.integers(-8, 9, (N, 1, 1))).astype(np.float32)).astype(BF))
    return d
def setup_inputs_zeros(rng):
    d = setup_inputs(rng); v = d["x"].reshape(N, 128, -1, 4).copy()
    v[np.broadcast_to((rng.random((N, 1, v.shape[2], 1)) < 0.33), v.shape)] = 0
    d["x"] = v.reshape(d["x"].shape)
    return d
def reference(gt, x, w1, w2):
    y = np.zeros((N, 128, NC), np.float32)
    for e in range(N):
        t = np.concatenate([x[j][:, 4 * OFF[j][e]:4 * OFF[j][e + 1]] for j in range(N)], axis=1)
        g = np.concatenate([gt[j][:, OFF[j][e]:OFF[j][e + 1]] for j in range(N)], axis=1).astype(np.float32)
        y[e] = mx_ref.matmul(mx_ref.quantize(w2[e]), mx_ref.quantize(tile(gated(layer(w1[e], [mx_ref.quantize(t)]), g))))
    return {"y": y}

from concourse.bass import DstId, RemoteDMATransfer
from concourse.mybir import dt, AluOpType, ActivationFunctionType

PADL, PADR = 32, 32
WB = PADL + 128 + PADR

SCRATCH = {
    "xt": ("sbuf", [128, 512], "bfloat16"),
    "w1t": ("sbuf", [128, 2048], "bfloat16"),
    "w2t": ("sbuf", [128, 512], "bfloat16"),
    "xq": ("sbuf", [128, 128], "float8_e4m3fn_x4"),
    "xs": ("sbuf", [128, 128], "uint8"),
    "w1q": ("sbuf", [128, 512], "float8_e4m3fn_x4"),
    "w1s": ("sbuf", [128, 512], "uint8"),
    "w2q": ("sbuf", [128, 128], "float8_e4m3fn_x4"),
    "w2s": ("sbuf", [128, 128], "uint8"),
    "bq": ("sbuf", [128, WB], "float8_e4m3fn_x4"),
    "bs": ("sbuf", [128, WB], "uint8"),
    "gd": ("dram", [128, 2], "bfloat16"),
    "gl": ("dram", [8, 128, 2], "bfloat16"),
    "grow": ("sbuf", [128, 128], "bfloat16"),
    "gb": ("sbuf", [128, 128], "bfloat16"),
    "zg": ("sbuf", [128, 512], "float32"),
    "h": ("sbuf", [128, 512], "bfloat16"),
    "hq": ("sbuf", [128, 128], "float8_e4m3fn_x4"),
    "hs": ("sbuf", [128, 128], "uint8"),
    "yt": ("sbuf", [128, 128], "float32"),
    "pz": ("psum", [128, 2048], "float32"),
    "py": ("psum", [128, 512], "float32"),
}
SEMAPHORES = ["gt", "x", "w1", "w2", "qx", "qw1", "qw2", "arr", "garr", "loc", "gat", "bc",
              "m0", "m1", "m2", "m3", "v0", "v1", "v2", "v3", "act", "qh", "my", "cp", "st"]


def bits(m):
    return [i for i in range(16) if m >> i & 1]


def plan(cnt, j):
    n = len(cnt)
    runs = []
    for e in range(n):
        c = cnt[j][e]
        if c and e != j:
            at = PADL + sum(cnt[i][e] for i in range(j))
            left = not any(cnt[i][e] for i in range(j))
            right = not any(cnt[i][e] for i in range(j + 1, n))
            runs.append((e, sum(cnt[j][:e]), c, at, left, right))

    def widen(r, w):
        e, a, c, at, left, right = r
        p = w - c
        if p == 0:
            return (e, a, c, at)
        if p < 0:
            return None
        if left and p <= PADL and a - p >= 0:
            return (e, a - p, w, at - p)
        if right and p <= PADR and a + w <= 128:
            return (e, a, w, at)
        return None

    groups = []
    while runs:
        best = None
        for w in sorted(set(r[2] for r in runs)):
            fit = [r for r in runs if widen(r, w)]
            score = (len(fit), -sum(w - r[2] for r in fit))
            if best is None or score > best[0]:
                best = (score, w, fit)
        groups.append([widen(r, best[1]) for r in best[2]])
        runs = [r for r in runs if r not in best[2]]
    calls = {}
    for kind, size in (("q", 4), ("s", 1)):
        for grp in groups:
            calls.setdefault(size * grp[0][2], []).extend((kind,) + r for r in grp)
    return sorted(calls.values(), key=lambda c: -len(c))


def shares(engines, k, flip):
    h = len(engines) // 2
    a, b = (engines[h:], engines[:h]) if flip else (engines[:h], engines[h:])

    def cut(s, m):
        w = len(s) // m
        return [s[w * i:w * i + w] for i in range(m)]
    if k in (1, 2, 4, 8):
        return cut(engines, k)
    if k == 3:
        return cut(a, 1) + cut(b, 2)
    if k == 5:
        return cut(a, 1) + cut(b, 4)
    return cut(a, 2) + cut(b, 4)[:k - 2]


def common(cnt, cores, j, topo):
    m = 0xFFFF
    for e in range(len(cores)):
        if e != j and cnt[j][e]:
            m &= topo.mask(cores[j], cores[e])
    return m


def routed(cnt, cores, j, topo):
    es, out, flips = bits(common(cnt, cores, j, topo)), [], {}
    for call in plan(cnt, j):
        k = len(call)
        flips[k] = not flips.get(k, True)
        out.append([(tr, sum(1 << i for i in s)) for tr, s in zip(call, shares(es, k, flips[k]))])
    return out


def rank_program(g, core, T, topo):
    me = T.rank_of(core)
    if me is None:
        return
    cnt, cores, S = T.tables["CNT"], T.cores, T.sem
    n = len(cores)
    dests = [e for e in range(n) if e != me and cnt[me][e]]
    froms = [j for j in range(n) if j != me and cnt[j][me]]
    v, t, act = g.vector, g.tensor, g.scalar

    g.sync.dma_start(T.gd[:], T.gt[0:2, :]).then_inc(S.gt, 16)
    act.dma_start(T.xt[:], T.x[:]).then_inc(S.x, 16)
    act.dma_start(T.w1t[:], T.w1[:]).then_inc(S.w1, 16)
    act.dma_start(T.w2t[:], T.w2[:]).then_inc(S.w2, 16)

    v.wait_ge(S.x, 16)
    v.quantize_mx(T.xq[:], T.xs[:], T.xt[:]).then_inc(S.qx, 1)
    v.wait_ge(S.w1, 16)
    v.quantize_mx(T.w1q[:], T.w1s[:], T.w1t[:]).then_inc(S.qw1, 1)
    v.wait_ge(S.w2, 16)
    v.quantize_mx(T.w2q[:], T.w2s[:], T.w2t[:]).then_inc(S.qw2, 1)

    sent = 0
    gm = common(cnt, cores, me, topo)
    ids = []
    for e in dests:
        rid, pid = topo.addr(cores[e], core)
        ids.append(DstId(rid=rid, pnc=pid))
    g.wait_ge(S.gt, 16)
    g.remote_dma_fused([RemoteDMATransfer(dst_ids=ids, dma_engine_mask=gm, remote_sem=S.garr,
                                          srcs=[T.gd[:]], dsts=[T.gl[me] for e in dests])], local_sem=S.loc)
    sent += len(bits(gm))

    g.wait_ge(S.qx, 1)
    for call in routed(cnt, cores, me, topo):
        trs = []
        for (kind, e, a, w, at), mk in call:
            rid, pid = topo.addr(cores[e], core)
            if kind == "q":
                src, dst = T.xq[:, a:a + w].bitcast(dt.uint8), T.bq[:, at:at + w].bitcast(dt.uint8)
            else:
                src, dst = T.xs[:, a:a + w], T.bs[:, at:at + w]
            trs.append((src, dst, rid, pid, mk))
            sent += len(bits(mk))
        if len(trs) == 1:
            src, dst, rid, pid, mk = trs[0]
            g.remote_dma(dst, src, S.arr, S.loc, pid, rid, mk)
        else:
            g.remote_dma_fused([RemoteDMATransfer(dst_ids=[DstId(rid=rid, pnc=pid)], dma_engine_mask=mk, remote_sem=S.arr,
                                                  src=src, dst=dst) for src, dst, rid, pid, mk in trs], local_sem=S.loc)

    garr = sum(len(bits(common(cnt, cores, j, topo))) for j in froms)
    g.sync.wait_ge(S.garr, garr)
    act.wait_ge(S.garr, garr)
    at = 0
    for k, j in enumerate(froms):
        a, c = sum(cnt[j][:me]), cnt[j][me]
        (g.sync, act)[k % 2].dma_start(T.grow[0:1, at:at + c], T.gl[j, a // 2:(a + c) // 2, :]).then_inc(S.gat, 16)
        at += c
    g.wait_ge(S.gat, 16 * len(froms))
    g.partition_broadcast(T.gb[:], T.grow[0:1, :], 128).then_inc(S.bc, 1)

    arr = sum(len(bits(mk)) for j in froms for call in routed(cnt, cores, j, topo) for tr, mk in call if tr[1] == me)
    t.wait_ge(S.qw1, 1)
    t.wait_ge(S.arr, arr)
    for i in range(4):
        t.matmul_mx(T.pz[:, 512 * i:512 * i + 128], T.w1q[:, 128 * i:128 * i + 128], T.w1s[:, 128 * i:128 * i + 128],
                    T.bq[:, PADL:PADL + 128], T.bs[:, PADL:PADL + 128], True, True).then_inc(S["m%d" % i], 1)
    v.wait_ge(S.bc, 1)
    for i in range(4):
        v.wait_ge(S["m%d" % i], 1)
        v.tensor_tensor(T.zg[:, 128 * i:128 * i + 128], T.pz[:, 512 * i:512 * i + 128], T.gb[:], AluOpType.mult
                        ).then_inc(S["v%d" % i], 1)
        act.wait_ge(S["v%d" % i], 1)
        act.activation(T.h[:, i:512:4], T.zg[:, 128 * i:128 * i + 128], ActivationFunctionType.Relu, scale=2.0 ** -4
                       ).then_inc(S.act, 1)
    v.wait_ge(S.act, 4)
    v.quantize_mx(T.hq[:], T.hs[:], T.h[:]).then_inc(S.qh, 1)
    t.wait_ge(S.qw2, 1)
    t.wait_ge(S.qh, 1)
    t.matmul_mx(T.py[:, 0:128], T.w2q[:], T.w2s[:], T.hq[:], T.hs[:], True, True).then_inc(S.my, 1)
    v.wait_ge(S.my, 1)
    v.tensor_copy(T.yt[:], T.py[:, 0:128]).then_inc(S.cp, 1)
    g.sync.wait_ge(S.cp, 1)
    g.sync.dma_start(T.y[:], T.yt[:]).then_inc(S.st, 16)
    g.sync.wait_ge(S.st, 16)
    g.wait_ge(S.loc, sent)
